import numpy as np
import ml_dtypes


def mxq(x, axis, fmt="e4m3"):
    dtype, down = {"e4m3": (ml_dtypes.float8_e4m3fn, 7), "e5m2": (ml_dtypes.float8_e5m2, 14)}[fmt]
    v = np.moveaxis(np.asarray(x, np.float32).astype(ml_dtypes.bfloat16).astype(np.float64), axis, -1)
    blocks = v.reshape(v.shape[:-1] + (-1, 32))
    amax = np.abs(blocks).max(-1, keepdims=True)
    byte = np.maximum(np.where(amax > 0, np.frexp(amax)[1] - 1 + 127, 0) - down, 1)
    scale = np.exp2(byte - 127.0)
    codes = (blocks / scale).astype(np.float32).astype(dtype).astype(np.float64)
    return np.moveaxis((codes * scale).reshape(v.shape), -1, axis)


WIDE = False


def mx_kscale(k):
    if not WIDE:
        return np.ones(k)
    levels = np.array([10, -10, 5, -5, 0])
    if k % 512:
        return np.exp2(np.random.permutation(np.resize(levels, k // 32))).repeat(32)
    a = np.empty((k // 512, 16))
    for p in range(k // 512):
        a[p, :8] = np.random.permutation(np.resize(levels, 8))
        for g in range(8):
            far = levels[np.abs(levels - a[p, g]) >= 10]
            a[p, g + 8] = far[np.random.randint(len(far))]
    return np.exp2(a.ravel()).repeat(32)


def f64(x):
    return np.asarray(x).astype(np.float64)


def striped(idx):
    return np.tile(np.asarray(idx).reshape(-1, 16).T, (8, 1)).astype(np.uint16)


def unstriped(offs):
    return offs[:16].T.reshape(-1).astype(np.int64)


E2M1 = np.array([0.0, 0.5, 1.0, 1.5, 2.0, 3.0, 4.0, 6.0, -0.0, -0.5, -1.0, -1.5, -2.0, -3.0, -4.0, -6.0])


def pack_weight(w, fmt):
    k, n = w.shape
    w = f64(np.asarray(w, np.float32).astype(ml_dtypes.bfloat16)).reshape(k // 32, 32, n)
    amax = np.abs(w).max(1)
    if fmt == "e4m3":
        byte = np.frexp(amax)[1] - 1 + 127 - 7
    else:
        mant, ex = np.frexp(amax / 6.0)
        byte = np.where(mant > 0.5, ex, ex - 1) + 127
    byte = np.clip(np.where(amax > 0, byte, 1), 1, 254)
    scaled = (w * np.exp2(127.0 - byte)[:, None, :]).reshape(k, n).astype(np.float32)
    by_word = np.ascontiguousarray(scaled.reshape(k // 512, 128, 4, n).transpose(0, 1, 3, 2))
    if fmt == "e4m3":
        words = by_word.astype(ml_dtypes.float8_e4m3fn).view(np.uint8)
    else:
        c = by_word.astype(ml_dtypes.float4_e2m1fn).view(np.uint8) & 0xF
        words = (c[..., 0::2] | (c[..., 1::2] << 4)).reshape(k // 512, 128, 2 * n)
    return np.ascontiguousarray(words), np.ascontiguousarray(byte.astype(np.uint8).reshape(k // 512, 16, n))


def unpack_weight(words, scales, fmt):
    g, _, n = scales.shape
    words = np.ascontiguousarray(words).reshape(g, 128, n, -1)
    if fmt == "e4m3":
        vals = words.view(ml_dtypes.float8_e4m3fn).astype(np.float64)
    else:
        nib = np.empty((g, 128, n, 4), np.uint8)
        nib[..., 0::2] = words & 0xF
        nib[..., 1::2] = words >> 4
        vals = E2M1[nib]
    vals = vals * np.repeat(np.exp2(scales.astype(np.float64) - 127.0), 8, axis=1)[..., None]
    return vals.transpose(0, 1, 3, 2).reshape(g * 512, n)


D, E, T, I, Q = 512, 512, 2048, 512, 128


def setup_inputs():
    n = np.random.standard_normal
    idx = np.random.permutation(T)[:I]
    fd = mx_kscale(D)
    fi = mx_kscale(I)
    ti = np.ones(T)
    ti[idx] = fi
    keysp = pack_weight(n((D, T)) / fd[:, None], "e2m1")
    return {
        "query": (n((D, Q)) * 0.4 / np.sqrt(D) * fd[:, None]).astype(np.float32),
        "keys_words": keysp[0],
        "keys_scales": keysp[1],
        "gain": (np.random.uniform(0.3, 0.8, (Q, 1))).astype(np.float32),
        "dquery": (n((D, Q)) * 0.6 / np.sqrt(D) * fd[:, None]).astype(np.float32),
        "os": (np.random.uniform(4.0, 16.0, (1, I)) * fi).astype(np.float32),
        "vals": (n((E, T)) / ti).astype(np.float32),
        "offs": striped(idx),
    }


def reference(query, keys_words, keys_scales, gain, dquery, os, vals, offs):
    idx = unstriped(offs)
    keysu = unpack_weight(keys_words, keys_scales, "e2m1")
    queryq = mxq(f64(query), 0, "e4m3")
    keysidxg = keysu[:, idx]
    a = queryq.T @ keysidxg
    dqueryq = mxq(f64(dquery), 0, "e4m3")
    ta = dqueryq.T @ keysidxg
    p = np.exp(a - np.max(a, axis=1, keepdims=True))
    z = np.sum(p, axis=1, keepdims=True)
    u1 = p / z * f64(gain) * 512.0
    p2 = np.exp(u1 - np.max(u1, axis=1, keepdims=True))
    z2 = np.sum(p2, axis=1, keepdims=True)
    tp = ta * p
    tz = np.sum(tp, axis=1, keepdims=True)
    tu1 = (tp - tz * p / z) / z * f64(gain) * 512.0
    tp2 = tu1 * p2
    tz2 = np.sum(tp2, axis=1, keepdims=True)
    tw = (tp2 - tz2 * p2 / z2) / z2
    wo1 = tw * f64(os)
    wt1 = wo1.T
    vt1 = f64(vals)[:, idx].T
    wt1q = mxq(wt1, 0, "e4m3")
    vt1q = mxq(vt1, 0, "e4m3")
    o = wt1q.T @ vt1q
    return o

@@ -1,0 +1,191 @@
+from contextlib import ExitStack
+
+import concourse.mybir as mybir
+from concourse.masks import make_identity
+
+F32 = mybir.dt.float32
+BF16 = mybir.dt.bfloat16
+I32 = mybir.dt.int32
+U32 = mybir.dt.uint32
+U16 = mybir.dt.uint16
+U8 = mybir.dt.uint8
+FP8X4 = mybir.dt.float8_e4m3fn_x4
+FP4X4 = mybir.dt.float4_e2m1fn_x4
+ALU = mybir.AluOpType
+ACT = mybir.ActivationFunctionType
+AXIS = mybir.AxisListType
+
+P = 128
+PACK = 4
+FEATURES = 512
+VALUE_FEATURES = 512
+TOKENS = 2048
+SLOTS = 512
+ROWS = 128
+VALUE_BLOCKS = VALUE_FEATURES // P
+HALF = VALUE_FEATURES // 2
+
+FLOPS = 2 * (2 * FEATURES * ROWS * SLOTS + SLOTS * ROWS * VALUE_FEATURES)
+
+
+def tile_attend_ttdoubled_kernel(tc, query, keys_words, keys_scales, gain, dquery, factors, vals, offs, out):
+    nc = tc.nc
+    with ExitStack() as ctx:
+        sb = ctx.enter_context(tc.tile_pool(name="sb", bufs=1))
+        ps = ctx.enter_context(tc.psum_pool(name="ps", bufs=1))
+        ps2 = ctx.enter_context(tc.psum_pool(name="ps2", bufs=2))
+
+        offsets = sb.tile([P, SLOTS // 16], U16, name="offsets")
+        nc.sync.dma_start(offsets[:], offs)
+        key_scale_pool = sb.tile([P, TOKENS], U8, name="key_scale_pool", align_bytes=64)
+        nc.gpsimd.memset(key_scale_pool[:].bitcast(I32), 0)
+        key_word_pool = sb.tile([P, TOKENS], U16, name="key_word_pool", align_bytes=64)
+        nc.sync.dma_start(key_word_pool[:].bitcast(I32), keys_words[0].bitcast(I32))
+        for quad in range(4):
+            nc.sync.dma_start(
+                key_scale_pool[32 * quad : 32 * quad + 4, :].bitcast(I32),
+                keys_scales[0, 4 * quad : 4 * quad + 4, :].bitcast(I32),
+            )
+        q_raw = sb.tile([P, PACK, ROWS], F32, name="q_raw")
+        nc.sync.dma_start(q_raw[:], query.rearrange("(p j) q -> p j q", j=PACK))
+        dq_raw = sb.tile([P, PACK, ROWS], F32, name="dq_raw")
+        nc.sync.dma_start(dq_raw[:], dquery.rearrange("(p j) q -> p j q", j=PACK))
+        val_pools = []
+        for b in range(VALUE_BLOCKS):
+            val_pool = sb.tile([P, TOKENS], F32, name="val_pool%d" % b, tag="val_pool%d" % b, align_bytes=64)
+            nc.sync.dma_start(val_pool[:], vals[b * P : (b + 1) * P, :])
+            val_pools.append(val_pool)
+            if b == 0:
+                gain_col = sb.tile([P, 1], F32, name="gain_col")
+                nc.sync.dma_start(gain_col[:], gain)
+                slot_factor = sb.tile([P, PACK], F32, name="slot_factor")
+                nc.sync.dma_start(slot_factor[:], factors.rearrange("o (p t) -> (o p) t", t=PACK))
+        ident = sb.tile([P, P], F32, name="ident")
+        make_identity(nc, ident[:])
+
+        warm = sb.tile([P, 1], F32, name="warm")
+        nc.vector.memset(warm[:], 0.0)
+        warm_out = sb.tile([P, 1], F32, name="warm_out")
+        nc.scalar.activation(warm_out[:], warm[:], ACT.Exp)
+
+        key_words = sb.tile([P, SLOTS], U16, name="key_words", align_bytes=64)
+        nc.vector.tensor_copy(key_words[:], key_word_pool[:].indirect(offsets[:]))
+        key_scales = sb.tile([P, SLOTS], U8, name="key_scales", align_bytes=64)
+        nc.vector.tensor_copy(key_scales[:], key_scale_pool[:].indirect(offsets[:]))
+
+        q_bf = sb.tile([P, 2, ROWS, PACK], BF16, name="q_bf", align_bytes=64)
+        for n, raw in enumerate((q_raw, dq_raw)):
+            nc.scalar.copy(q_bf[:, n], raw[:].rearrange("p j q -> p q j"))
+        q_codes = sb.tile([P, 2 * ROWS], U32, name="q_codes", align_bytes=64)
+        q_scales = sb.tile([P, 2 * ROWS], U8, name="q_scales", align_bytes=64)
+        nc.vector.quantize_mx(q_codes[:].bitcast(FP8X4), q_scales[:], q_bf[:].rearrange("p n q j -> p (n q j)"))
+
+        score_banks = []
+        for n in range(2):
+            bank = ps.tile([P, SLOTS], F32, name="score%d" % n)
+            nc.tensor.matmul_mx(
+                bank[:],
+                lhsT=q_codes[:, n * ROWS : (n + 1) * ROWS].bitcast(FP8X4),
+                lhsT_scale=q_scales[:, n * ROWS : (n + 1) * ROWS],
+                rhs=key_words[:].bitcast(FP4X4),
+                rhs_scale=key_scales[:],
+                start=True,
+                stop=True,
+            )
+            score_banks.append(bank)
+        a_dealt = score_banks[0][:].rearrange("p (s t) -> p t s", t=PACK)
+        ta_dealt = score_banks[1][:].rearrange("p (s t) -> p t s", t=PACK)
+
+        val_codes = sb.tile([P, VALUE_FEATURES], U32, name="val_codes", align_bytes=64)
+        val_scales = sb.tile([P, VALUE_FEATURES], U8, name="val_scales", align_bytes=64)
+
+        val_bf = [sb.tile([P, HALF * PACK], BF16, name="val_bf%d" % h, align_bytes=64) for h in range(2)]
+
+        def gather_values(b):
+            picked = sb.tile([P, SLOTS], BF16, name="picked%d" % b, align_bytes=64)
+            nc.vector.tensor_copy(picked[:], val_pools[b][:].indirect(offsets[:]))
+            pairs = picked[:].bitcast(F32)
+            turned = ps2.tile([P, 2, P], F32, name="turned")
+            for u in range(2):
+                nc.tensor.transpose(turned[:, u, :], pairs[:, u : SLOTS // 2 : 2], ident[:])
+            words = val_bf[b // 2][:, (b % 2) * P * PACK : (b % 2 + 1) * P * PACK].bitcast(F32)
+            nc.scalar.copy(words.rearrange("p (e u) -> p e u", u=2), turned[:].rearrange("p u e -> p e u"))
+
+        def quantize_values(h):
+            cols = slice(h * HALF, (h + 1) * HALF)
+            nc.vector.quantize_mx(val_codes[:, cols].bitcast(FP8X4), val_scales[:, cols], val_bf[h][:])
+
+        def column(name):
+            return sb.tile([P, 1], F32, name=name)
+
+        def dealt(name):
+            return sb.tile([P, PACK, P], F32, name=name)
+
+        neg_max = column("neg_max")
+        nc.vector.tensor_reduce(neg_max[:], score_banks[0][:], AXIS.X, ALU.max, negate=True)
+        p1 = dealt("p1")
+        z1 = column("z1")
+        nc.scalar.activation(p1[:], a_dealt, ACT.Exp, bias=neg_max[:], scale=1.0, accum_out=z1[:])
+        gather_values(0)
+        inv_z1 = column("inv_z1")
+        nc.vector.reciprocal(inv_z1[:], z1[:])
+        neg_c = column("neg_c")
+        nc.vector.tensor_scalar(neg_c[:], inv_z1[:], gain_col[:], -float(SLOTS), ALU.mult, ALU.mult)
+        neg_u1 = dealt("neg_u1")
+        neg_max2 = column("neg_max2")
+        nc.vector.tensor_scalar(neg_u1[:], p1[:], neg_c[:], None, ALU.mult, ALU.min, accum_out=neg_max2[:])
+        p2 = dealt("p2")
+        z2 = column("z2")
+        nc.scalar.activation(p2[:], neg_u1[:], ACT.Exp, bias=neg_max2[:], scale=-1.0, accum_out=z2[:])
+        tp_over_z = dealt("tp_over_z")
+        mean_ta = column("mean_ta")
+        nc.vector.scalar_tensor_tensor(
+            tp_over_z[:], ta_dealt, inv_z1[:], p1[:], ALU.mult, ALU.mult, accum_out=mean_ta[:]
+        )
+        neg_tu1 = dealt("neg_tu1")
+        nc.vector.scalar_tensor_tensor(neg_tu1[:], ta_dealt, mean_ta[:], neg_u1[:], ALU.subtract, ALU.mult)
+        inv_z2 = column("inv_z2")
+        nc.vector.reciprocal(inv_z2[:], z2[:])
+        gather_values(1)
+        neg_tp2 = dealt("neg_tp2")
+        neg_mean = column("neg_mean")
+        nc.vector.scalar_tensor_tensor(
+            neg_tp2[:], neg_tu1[:], inv_z2[:], p2[:], ALU.mult, ALU.mult, accum_out=neg_mean[:]
+        )
+        quantize_values(0)
+        shift = column("shift")
+        nc.vector.tensor_tensor(shift[:], neg_mean[:], inv_z2[:], ALU.mult)
+        tw = dealt("tw")
+        nc.vector.scalar_tensor_tensor(tw[:], p2[:], shift[:], neg_tp2[:], ALU.mult, ALU.subtract)
+        tw_turned = ps.tile([P, PACK, ROWS], F32, name="tw_turned")
+        for t in range(PACK):
+            nc.tensor.transpose(tw_turned[:, t, :], tw[:, t, :], ident[:])
+        gather_values(2)
+        gather_values(3)
+        w_bf = sb.tile([P, ROWS, PACK], BF16, name="w_bf", tag="val_pool3", align_bytes=64)
+        nc.vector.tensor_tensor(
+            w_bf[:],
+            tw_turned[:].rearrange("p t q -> p q t"),
+            slot_factor[:].unsqueeze(1).to_broadcast([P, ROWS, PACK]),
+            ALU.mult,
+        )
+        w_codes = sb.tile([P, ROWS], U32, name="w_codes", align_bytes=64)
+        w_scales = sb.tile([P, ROWS], U8, name="w_scales", align_bytes=64)
+        nc.vector.quantize_mx(w_codes[:].bitcast(FP8X4), w_scales[:], w_bf[:].rearrange("p q t -> p (q t)"))
+        quantize_values(1)
+
+        for h in range(2):
+            cols = slice(h * HALF, (h + 1) * HALF)
+            acc = ps.tile([P, HALF], F32, name="acc%d" % h)
+            nc.tensor.matmul_mx(
+                acc[:],
+                lhsT=w_codes[:].bitcast(FP8X4),
+                lhsT_scale=w_scales[:],
+                rhs=val_codes[:, cols].bitcast(FP8X4),
+                rhs_scale=val_scales[:, cols],
+                start=True,
+                stop=True,
+            )
+            result = sb.tile([P, HALF], F32, name="result%d" % h)
+            nc.scalar.copy(result[:], acc[:])
+            nc.sync.dma_start(out[:, cols], result[:])

@@ -24,6 +24,7 @@ SLOTS = 512
 ROWS = 128
 VALUE_BLOCKS = VALUE_FEATURES // P
 HALF = VALUE_FEATURES // 2
+HALF_SLOTS = SLOTS // 2
 
 FLOPS = 2 * (2 * FEATURES * ROWS * SLOTS + SLOTS * ROWS * VALUE_FEATURES)
 
@@ -33,7 +34,6 @@ def tile_attend_ttdoubled_kernel(tc, query, keys_words, keys_scales, gain, dquer
     with ExitStack() as ctx:
         sb = ctx.enter_context(tc.tile_pool(name="sb", bufs=1))
         ps = ctx.enter_context(tc.psum_pool(name="ps", bufs=1))
-        ps2 = ctx.enter_context(tc.psum_pool(name="ps2", bufs=2))
 
         offsets = sb.tile([P, SLOTS // 16], U16, name="offsets")
         nc.sync.dma_start(offsets[:], offs)
@@ -50,15 +50,15 @@ def tile_attend_ttdoubled_kernel(tc, query, keys_words, keys_scales, gain, dquer
         nc.sync.dma_start(q_raw[:], query.rearrange("(p j) q -> p j q", j=PACK))
         dq_raw = sb.tile([P, PACK, ROWS], F32, name="dq_raw")
         nc.sync.dma_start(dq_raw[:], dquery.rearrange("(p j) q -> p j q", j=PACK))
-        val_pools = []
-        for b in range(VALUE_BLOCKS):
+        val_pools = {}
+        for b in (2, 0, 1, 3):
             val_pool = sb.tile([P, TOKENS], F32, name="val_pool%d" % b, tag="val_pool%d" % b, align_bytes=64)
             nc.sync.dma_start(val_pool[:], vals[b * P : (b + 1) * P, :])
-            val_pools.append(val_pool)
-            if b == 0:
+            val_pools[b] = val_pool
+            if b == 2:
                 gain_col = sb.tile([P, 1], F32, name="gain_col")
                 nc.sync.dma_start(gain_col[:], gain)
-                slot_factor = sb.tile([P, PACK], F32, name="slot_factor")
+                slot_factor = sb.tile([P, PACK], F32, name="slot_factor", tag="slot_factor", align_bytes=64)
                 nc.sync.dma_start(slot_factor[:], factors.rearrange("o (p t) -> (o p) t", t=PACK))
         ident = sb.tile([P, P], F32, name="ident")
         make_identity(nc, ident[:])
@@ -68,71 +68,111 @@ def tile_attend_ttdoubled_kernel(tc, query, keys_words, keys_scales, gain, dquer
         warm_out = sb.tile([P, 1], F32, name="warm_out")
         nc.scalar.activation(warm_out[:], warm[:], ACT.Exp)
 
-        key_words = sb.tile([P, SLOTS], U16, name="key_words", align_bytes=64)
-        nc.vector.tensor_copy(key_words[:], key_word_pool[:].indirect(offsets[:]))
-        key_scales = sb.tile([P, SLOTS], U8, name="key_scales", align_bytes=64)
-        nc.vector.tensor_copy(key_scales[:], key_scale_pool[:].indirect(offsets[:]))
+        def quantize_query(name, raw):
+            rounded = sb.tile([P, ROWS, PACK], BF16, name=name + "_bf", tag=name + "_bf", align_bytes=64)
+            nc.scalar.copy(rounded[:], raw[:].rearrange("p j q -> p q j"))
+            codes = sb.tile([P, ROWS], U32, name=name + "_codes", tag=name + "_codes", align_bytes=64)
+            scales = sb.tile([P, ROWS], U8, name=name + "_scales", align_bytes=64)
+            nc.vector.quantize_mx(codes[:].bitcast(FP8X4), scales[:], rounded[:].rearrange("p q j -> p (q j)"))
+            return codes, scales
 
-        q_bf = sb.tile([P, 2, ROWS, PACK], BF16, name="q_bf", align_bytes=64)
-        for n, raw in enumerate((q_raw, dq_raw)):
-            nc.scalar.copy(q_bf[:, n], raw[:].rearrange("p j q -> p q j"))
-        q_codes = sb.tile([P, 2 * ROWS], U32, name="q_codes", align_bytes=64)
-        q_scales = sb.tile([P, 2 * ROWS], U8, name="q_scales", align_bytes=64)
-        nc.vector.quantize_mx(q_codes[:].bitcast(FP8X4), q_scales[:], q_bf[:].rearrange("p n q j -> p (n q j)"))
-
-        score_banks = []
-        for n in range(2):
-            bank = ps.tile([P, SLOTS], F32, name="score%d" % n)
+        def scores(dest, operand, h):
             nc.tensor.matmul_mx(
-                bank[:],
-                lhsT=q_codes[:, n * ROWS : (n + 1) * ROWS].bitcast(FP8X4),
-                lhsT_scale=q_scales[:, n * ROWS : (n + 1) * ROWS],
-                rhs=key_words[:].bitcast(FP4X4),
-                rhs_scale=key_scales[:],
+                dest,
+                lhsT=operand[0][:].bitcast(FP8X4),
+                lhsT_scale=operand[1][:],
+                rhs=key_words[h][:].bitcast(FP4X4),
+                rhs_scale=key_scales[h][:],
                 start=True,
                 stop=True,
             )
-            score_banks.append(bank)
-        a_dealt = score_banks[0][:].rearrange("p (s t) -> p t s", t=PACK)
-        ta_dealt = score_banks[1][:].rearrange("p (s t) -> p t s", t=PACK)
 
-        val_codes = sb.tile([P, VALUE_FEATURES], U32, name="val_codes", align_bytes=64)
-        val_scales = sb.tile([P, VALUE_FEATURES], U8, name="val_scales", align_bytes=64)
+        def column(name, tag=""):
+            return sb.tile([P, 1], F32, name=name, tag=tag or name, align_bytes=64)
+
+        def dealt(name, tag=""):
+            return sb.tile([P, PACK, P], F32, name=name, tag=tag or name, align_bytes=64)
+
+        q_mx = quantize_query("q", q_raw)
+        key_words, key_scales = [], []
+        neg_a = dealt("neg_a")
+        neg_max = None
+        for h in range(2):
+            half_list = offsets[:, h * HALF_SLOTS // 16 : (h + 1) * HALF_SLOTS // 16]
+            words = sb.tile([P, HALF_SLOTS], U16, name="key_words%d" % h, align_bytes=64)
+            nc.vector.tensor_copy(words[:], key_word_pool[:].indirect(half_list))
+            scales = sb.tile(
+                [P, HALF_SLOTS], U8, name="key_scales%d" % h, tag=("key_scales0", "q_bf")[h], align_bytes=64
+            )
+            nc.vector.tensor_copy(scales[:], key_scale_pool[:].indirect(half_list))
+            key_words.append(words)
+            key_scales.append(scales)
+        for h in range(2):
+            bank = ps.tile([P, HALF_SLOTS], F32, name="score%d" % h, tag="score%d" % h)
+            scores(bank[:], q_mx, h)
+            so_far = neg_max
+            neg_max = column("neg_max%d" % h)
+            nc.vector.tensor_scalar(
+                neg_a[:, :, h * HALF_SLOTS // PACK : (h + 1) * HALF_SLOTS // PACK],
+                bank[:].rearrange("p (s t) -> p t s", t=PACK),
+                -1.0,
+                so_far[:] if h else None,
+                ALU.mult,
+                ALU.min,
+                accum_out=neg_max[:],
+            )
+        p1 = dealt("p1")
+        z1 = column("z1")
+        nc.scalar.activation(p1[:], neg_a[:], ACT.Exp, bias=neg_max[:], scale=-1.0, accum_out=z1[:])
+        dq_mx = quantize_query("dq", dq_raw)
+        ta_bank = ps.tile([P, SLOTS], F32, name="ta_bank")
+        for h in range(2):
+            scores(ta_bank[:, h * HALF_SLOTS : (h + 1) * HALF_SLOTS], dq_mx, h)
+        ta_dealt = ta_bank[:].rearrange("p (s t) -> p t s", t=PACK)
+
 
         val_bf = [sb.tile([P, HALF * PACK], BF16, name="val_bf%d" % h, align_bytes=64) for h in range(2)]
 
-        def gather_values(b):
-            picked = sb.tile([P, SLOTS], BF16, name="picked%d" % b, align_bytes=64)
-            nc.vector.tensor_copy(picked[:], val_pools[b][:].indirect(offsets[:]))
-            pairs = picked[:].bitcast(F32)
-            turned = ps2.tile([P, 2, P], F32, name="turned")
-            for u in range(2):
-                nc.tensor.transpose(turned[:, u, :], pairs[:, u : SLOTS // 2 : 2], ident[:])
-            words = val_bf[b // 2][:, (b % 2) * P * PACK : (b % 2 + 1) * P * PACK].bitcast(F32)
-            nc.scalar.copy(words.rearrange("p (e u) -> p e u", u=2), turned[:].rearrange("p u e -> p e u"))
+        picked_tiles = {}
+
+        def gather_values(b, after, on_scalar=False):
+            picked = sb.tile([P, SLOTS], BF16, name="picked%d" % b, tag=after, align_bytes=64)
+            if on_scalar:
+                rounded = sb.tile([P, TOKENS], BF16, name="rounded_pool", tag="neg_max_u1", align_bytes=64)
+                nc.scalar.activation(rounded[:], val_pools[b][:], ACT.Copy)
+                nc.scalar.activation(picked[:], rounded[:].indirect(offsets[:]), ACT.Copy)
+            else:
+                nc.vector.tensor_copy(picked[:], val_pools[b][:].indirect(offsets[:]))
+            picked_tiles[b] = picked
+
+        def turn_values(blocks, bank):
+            turned = ps.tile([P, len(blocks), 2, P], F32, name="turned%d" % blocks[0], tag=bank)
+            for b in blocks:
+                pairs = picked_tiles[b][:].bitcast(F32)
+                for u in range(2):
+                    nc.tensor.transpose(turned[:, b - min(blocks), u, :], pairs[:, u : SLOTS // 2 : 2], ident[:])
+            first = min(blocks)
+            words = val_bf[first // 2][:, (first % 2) * P * PACK : (first % 2 + len(blocks)) * P * PACK].bitcast(F32)
+            nc.scalar.copy(
+                words.rearrange("p (b e u) -> p b e u", u=2, e=P), turned[:].rearrange("p b u e -> p b e u")
+            )
 
         def quantize_values(h):
-            cols = slice(h * HALF, (h + 1) * HALF)
-            nc.vector.quantize_mx(val_codes[:, cols].bitcast(FP8X4), val_scales[:, cols], val_bf[h][:])
+            codes = sb.tile(
+                [P, HALF], U32, name="val_codes%d" % h, tag=("slot_factor", "val_codes1")[h], align_bytes=64
+            )
+            scales = sb.tile([P, HALF], U8, name="val_scales%d" % h, align_bytes=64)
+            nc.vector.quantize_mx(codes[:].bitcast(FP8X4), scales[:], val_bf[h][:])
+            return codes, scales
 
-        def column(name):
-            return sb.tile([P, 1], F32, name=name)
-
-        def dealt(name):
-            return sb.tile([P, PACK, P], F32, name=name)
-
-        neg_max = column("neg_max")
-        nc.vector.tensor_reduce(neg_max[:], score_banks[0][:], AXIS.X, ALU.max, negate=True)
-        p1 = dealt("p1")
-        z1 = column("z1")
-        nc.scalar.activation(p1[:], a_dealt, ACT.Exp, bias=neg_max[:], scale=1.0, accum_out=z1[:])
-        gather_values(0)
-        inv_z1 = column("inv_z1")
+        gather_values(2, "q_codes")
+        turn_values([2], "turn_a")
+        inv_z1 = column("inv_z1", tag="val_pool2")
         nc.vector.reciprocal(inv_z1[:], z1[:])
         neg_c = column("neg_c")
         nc.vector.tensor_scalar(neg_c[:], inv_z1[:], gain_col[:], -float(SLOTS), ALU.mult, ALU.mult)
         neg_u1 = dealt("neg_u1")
-        neg_max2 = column("neg_max2")
+        neg_max2 = column("neg_max_u1")
         nc.vector.tensor_scalar(neg_u1[:], p1[:], neg_c[:], None, ALU.mult, ALU.min, accum_out=neg_max2[:])
         p2 = dealt("p2")
         z2 = column("z2")
@@ -146,13 +186,12 @@ def tile_attend_ttdoubled_kernel(tc, query, keys_words, keys_scales, gain, dquer
         nc.vector.scalar_tensor_tensor(neg_tu1[:], ta_dealt, mean_ta[:], neg_u1[:], ALU.subtract, ALU.mult)
         inv_z2 = column("inv_z2")
         nc.vector.reciprocal(inv_z2[:], z2[:])
-        gather_values(1)
+        gather_values(0, "picked0", on_scalar=True)
         neg_tp2 = dealt("neg_tp2")
         neg_mean = column("neg_mean")
         nc.vector.scalar_tensor_tensor(
             neg_tp2[:], neg_tu1[:], inv_z2[:], p2[:], ALU.mult, ALU.mult, accum_out=neg_mean[:]
         )
-        quantize_values(0)
         shift = column("shift")
         nc.vector.tensor_tensor(shift[:], neg_mean[:], inv_z2[:], ALU.mult)
         tw = dealt("tw")
@@ -160,8 +199,10 @@ def tile_attend_ttdoubled_kernel(tc, query, keys_words, keys_scales, gain, dquer
         tw_turned = ps.tile([P, PACK, ROWS], F32, name="tw_turned")
         for t in range(PACK):
             nc.tensor.transpose(tw_turned[:, t, :], tw[:, t, :], ident[:])
-        gather_values(2)
-        gather_values(3)
+        gather_values(1, "picked1")
+        turn_values([1, 0], "score0")
+        gather_values(3, "picked3")
+        turn_values([3], "score1")
         w_bf = sb.tile([P, ROWS, PACK], BF16, name="w_bf", tag="val_pool3", align_bytes=64)
         nc.vector.tensor_tensor(
             w_bf[:],
@@ -172,7 +213,7 @@ def tile_attend_ttdoubled_kernel(tc, query, keys_words, keys_scales, gain, dquer
         w_codes = sb.tile([P, ROWS], U32, name="w_codes", align_bytes=64)
         w_scales = sb.tile([P, ROWS], U8, name="w_scales", align_bytes=64)
         nc.vector.quantize_mx(w_codes[:].bitcast(FP8X4), w_scales[:], w_bf[:].rearrange("p q t -> p (q t)"))
-        quantize_values(1)
+        val_mx = [quantize_values(h) for h in range(2)]
 
         for h in range(2):
             cols = slice(h * HALF, (h + 1) * HALF)
@@ -181,8 +222,8 @@ def tile_attend_ttdoubled_kernel(tc, query, keys_words, keys_scales, gain, dquer
                 acc[:],
                 lhsT=w_codes[:].bitcast(FP8X4),
                 lhsT_scale=w_scales[:],
-                rhs=val_codes[:, cols].bitcast(FP8X4),
-                rhs_scale=val_scales[:, cols],
+                rhs=val_mx[h][0][:].bitcast(FP8X4),
+                rhs_scale=val_mx[h][1][:],
                 start=True,
                 stop=True,
             )

from contextlib import ExitStack

import concourse.mybir as mybir
from concourse.masks import make_identity

F32 = mybir.dt.float32
BF16 = mybir.dt.bfloat16
I32 = mybir.dt.int32
U32 = mybir.dt.uint32
U16 = mybir.dt.uint16
U8 = mybir.dt.uint8
FP8X4 = mybir.dt.float8_e4m3fn_x4
FP4X4 = mybir.dt.float4_e2m1fn_x4
ALU = mybir.AluOpType
ACT = mybir.ActivationFunctionType
AXIS = mybir.AxisListType

P = 128
PACK = 4
FEATURES = 512
VALUE_FEATURES = 512
TOKENS = 2048
SLOTS = 512
ROWS = 128
VALUE_BLOCKS = VALUE_FEATURES // P
HALF = VALUE_FEATURES // 2
HALF_SLOTS = SLOTS // 2

FLOPS = 2 * (2 * FEATURES * ROWS * SLOTS + SLOTS * ROWS * VALUE_FEATURES)


def tile_attend_ttdoubled_kernel(tc, query, keys_words, keys_scales, gain, dquery, factors, vals, offs, out):
    nc = tc.nc
    with ExitStack() as ctx:
        sb = ctx.enter_context(tc.tile_pool(name="sb", bufs=1))
        ps = ctx.enter_context(tc.psum_pool(name="ps", bufs=1))

        offsets = sb.tile([P, SLOTS // 16], U16, name="offsets")
        nc.sync.dma_start(offsets[:], offs)
        key_scale_pool = sb.tile([P, TOKENS], U8, name="key_scale_pool", align_bytes=64)
        nc.gpsimd.memset(key_scale_pool[:].bitcast(I32), 0)
        key_word_pool = sb.tile([P, TOKENS], U16, name="key_word_pool", align_bytes=64)
        nc.sync.dma_start(key_word_pool[:].bitcast(I32), keys_words[0].bitcast(I32))
        for quad in range(4):
            nc.sync.dma_start(
                key_scale_pool[32 * quad : 32 * quad + 4, :].bitcast(I32),
                keys_scales[0, 4 * quad : 4 * quad + 4, :].bitcast(I32),
            )
        q_raw = sb.tile([P, PACK, ROWS], F32, name="q_raw")
        nc.sync.dma_start(q_raw[:], query.rearrange("(p j) q -> p j q", j=PACK))
        dq_raw = sb.tile([P, PACK, ROWS], F32, name="dq_raw")
        nc.sync.dma_start(dq_raw[:], dquery.rearrange("(p j) q -> p j q", j=PACK))
        val_pools = {}
        for b in (2, 0, 1, 3):
            val_pool = sb.tile([P, TOKENS], F32, name="val_pool%d" % b, tag="val_pool%d" % b, align_bytes=64)
            nc.sync.dma_start(val_pool[:], vals[b * P : (b + 1) * P, :])
            val_pools[b] = val_pool
            if b == 2:
                gain_col = sb.tile([P, 1], F32, name="gain_col")
                nc.sync.dma_start(gain_col[:], gain)
                slot_factor = sb.tile([P, PACK], F32, name="slot_factor", tag="slot_factor", align_bytes=64)
                nc.sync.dma_start(slot_factor[:], factors.rearrange("o (p t) -> (o p) t", t=PACK))
        ident = sb.tile([P, P], F32, name="ident")
        make_identity(nc, ident[:])

        warm = sb.tile([P, 1], F32, name="warm")
        nc.vector.memset(warm[:], 0.0)
        warm_out = sb.tile([P, 1], F32, name="warm_out")
        nc.scalar.activation(warm_out[:], warm[:], ACT.Exp)

        def quantize_query(name, raw):
            rounded = sb.tile([P, ROWS, PACK], BF16, name=name + "_bf", tag=name + "_bf", align_bytes=64)
            nc.scalar.copy(rounded[:], raw[:].rearrange("p j q -> p q j"))
            codes = sb.tile([P, ROWS], U32, name=name + "_codes", tag=name + "_codes", align_bytes=64)
            scales = sb.tile([P, ROWS], U8, name=name + "_scales", align_bytes=64)
            nc.vector.quantize_mx(codes[:].bitcast(FP8X4), scales[:], rounded[:].rearrange("p q j -> p (q j)"))
            return codes, scales

        def scores(dest, operand, h):
            nc.tensor.matmul_mx(
                dest,
                lhsT=operand[0][:].bitcast(FP8X4),
                lhsT_scale=operand[1][:],
                rhs=key_words[h][:].bitcast(FP4X4),
                rhs_scale=key_scales[h][:],
                start=True,
                stop=True,
            )

        def column(name, tag=""):
            return sb.tile([P, 1], F32, name=name, tag=tag or name, align_bytes=64)

        def dealt(name, tag=""):
            return sb.tile([P, PACK, P], F32, name=name, tag=tag or name, align_bytes=64)

        q_mx = quantize_query("q", q_raw)
        key_words, key_scales = [], []
        neg_a = dealt("neg_a")
        neg_max = None
        for h in range(2):
            half_list = offsets[:, h * HALF_SLOTS // 16 : (h + 1) * HALF_SLOTS // 16]
            words = sb.tile([P, HALF_SLOTS], U16, name="key_words%d" % h, align_bytes=64)
            nc.vector.tensor_copy(words[:], key_word_pool[:].indirect(half_list))
            scales = sb.tile(
                [P, HALF_SLOTS], U8, name="key_scales%d" % h, tag=("key_scales0", "q_bf")[h], align_bytes=64
            )
            nc.vector.tensor_copy(scales[:], key_scale_pool[:].indirect(half_list))
            key_words.append(words)
            key_scales.append(scales)
        for h in range(2):
            bank = ps.tile([P, HALF_SLOTS], F32, name="score%d" % h, tag="score%d" % h)
            scores(bank[:], q_mx, h)
            so_far = neg_max
            neg_max = column("neg_max%d" % h)
            nc.vector.tensor_scalar(
                neg_a[:, :, h * HALF_SLOTS // PACK : (h + 1) * HALF_SLOTS // PACK],
                bank[:].rearrange("p (s t) -> p t s", t=PACK),
                -1.0,
                so_far[:] if h else None,
                ALU.mult,
                ALU.min,
                accum_out=neg_max[:],
            )
        p1 = dealt("p1")
        z1 = column("z1")
        nc.scalar.activation(p1[:], neg_a[:], ACT.Exp, bias=neg_max[:], scale=-1.0, accum_out=z1[:])
        dq_mx = quantize_query("dq", dq_raw)
        ta_bank = ps.tile([P, SLOTS], F32, name="ta_bank")
        for h in range(2):
            scores(ta_bank[:, h * HALF_SLOTS : (h + 1) * HALF_SLOTS], dq_mx, h)
        ta_dealt = ta_bank[:].rearrange("p (s t) -> p t s", t=PACK)


        val_bf = [sb.tile([P, HALF * PACK], BF16, name="val_bf%d" % h, align_bytes=64) for h in range(2)]

        picked_tiles = {}

        def gather_values(b, after, on_scalar=False):
            picked = sb.tile([P, SLOTS], BF16, name="picked%d" % b, tag=after, align_bytes=64)
            if on_scalar:
                rounded = sb.tile([P, TOKENS], BF16, name="rounded_pool", tag="neg_max_u1", align_bytes=64)
                nc.scalar.activation(rounded[:], val_pools[b][:], ACT.Copy)
                nc.scalar.activation(picked[:], rounded[:].indirect(offsets[:]), ACT.Copy)
            else:
                nc.vector.tensor_copy(picked[:], val_pools[b][:].indirect(offsets[:]))
            picked_tiles[b] = picked

        def turn_values(blocks, bank):
            turned = ps.tile([P, len(blocks), 2, P], F32, name="turned%d" % blocks[0], tag=bank)
            for b in blocks:
                pairs = picked_tiles[b][:].bitcast(F32)
                for u in range(2):
                    nc.tensor.transpose(turned[:, b - min(blocks), u, :], pairs[:, u : SLOTS // 2 : 2], ident[:])
            first = min(blocks)
            words = val_bf[first // 2][:, (first % 2) * P * PACK : (first % 2 + len(blocks)) * P * PACK].bitcast(F32)
            nc.scalar.copy(
                words.rearrange("p (b e u) -> p b e u", u=2, e=P), turned[:].rearrange("p b u e -> p b e u")
            )

        def quantize_values(h):
            codes = sb.tile(
                [P, HALF], U32, name="val_codes%d" % h, tag=("slot_factor", "val_codes1")[h], align_bytes=64
            )
            scales = sb.tile([P, HALF], U8, name="val_scales%d" % h, align_bytes=64)
            nc.vector.quantize_mx(codes[:].bitcast(FP8X4), scales[:], val_bf[h][:])
            return codes, scales

        gather_values(2, "q_codes")
        turn_values([2], "turn_a")
        inv_z1 = column("inv_z1", tag="val_pool2")
        nc.vector.reciprocal(inv_z1[:], z1[:])
        neg_c = column("neg_c")
        nc.vector.tensor_scalar(neg_c[:], inv_z1[:], gain_col[:], -float(SLOTS), ALU.mult, ALU.mult)
        neg_u1 = dealt("neg_u1")
        neg_max2 = column("neg_max_u1")
        nc.vector.tensor_scalar(neg_u1[:], p1[:], neg_c[:], None, ALU.mult, ALU.min, accum_out=neg_max2[:])
        p2 = dealt("p2")
        z2 = column("z2")
        nc.scalar.activation(p2[:], neg_u1[:], ACT.Exp, bias=neg_max2[:], scale=-1.0, accum_out=z2[:])
        tp_over_z = dealt("tp_over_z")
        mean_ta = column("mean_ta")
        nc.vector.scalar_tensor_tensor(
            tp_over_z[:], ta_dealt, inv_z1[:], p1[:], ALU.mult, ALU.mult, accum_out=mean_ta[:]
        )
        neg_tu1 = dealt("neg_tu1")
        nc.vector.scalar_tensor_tensor(neg_tu1[:], ta_dealt, mean_ta[:], neg_u1[:], ALU.subtract, ALU.mult)
        inv_z2 = column("inv_z2")
        nc.vector.reciprocal(inv_z2[:], z2[:])
        gather_values(0, "picked0", on_scalar=True)
        neg_tp2 = dealt("neg_tp2")
        neg_mean = column("neg_mean")
        nc.vector.scalar_tensor_tensor(
            neg_tp2[:], neg_tu1[:], inv_z2[:], p2[:], ALU.mult, ALU.mult, accum_out=neg_mean[:]
        )
        shift = column("shift")
        nc.vector.tensor_tensor(shift[:], neg_mean[:], inv_z2[:], ALU.mult)
        tw = dealt("tw")
        nc.vector.scalar_tensor_tensor(tw[:], p2[:], shift[:], neg_tp2[:], ALU.mult, ALU.subtract)
        tw_turned = ps.tile([P, PACK, ROWS], F32, name="tw_turned")
        for t in range(PACK):
            nc.tensor.transpose(tw_turned[:, t, :], tw[:, t, :], ident[:])
        gather_values(1, "picked1")
        turn_values([1, 0], "score0")
        gather_values(3, "picked3")
        turn_values([3], "score1")
        w_bf = sb.tile([P, ROWS, PACK], BF16, name="w_bf", tag="val_pool3", align_bytes=64)
        nc.vector.tensor_tensor(
            w_bf[:],
            tw_turned[:].rearrange("p t q -> p q t"),
            slot_factor[:].unsqueeze(1).to_broadcast([P, ROWS, PACK]),
            ALU.mult,
        )
        w_codes = sb.tile([P, ROWS], U32, name="w_codes", align_bytes=64)
        w_scales = sb.tile([P, ROWS], U8, name="w_scales", align_bytes=64)
        nc.vector.quantize_mx(w_codes[:].bitcast(FP8X4), w_scales[:], w_bf[:].rearrange("p q t -> p (q t)"))
        val_mx = [quantize_values(h) for h in range(2)]

        for h in range(2):
            cols = slice(h * HALF, (h + 1) * HALF)
            acc = ps.tile([P, HALF], F32, name="acc%d" % h)
            nc.tensor.matmul_mx(
                acc[:],
                lhsT=w_codes[:].bitcast(FP8X4),
                lhsT_scale=w_scales[:],
                rhs=val_mx[h][0][:].bitcast(FP8X4),
                rhs_scale=val_mx[h][1][:],
                start=True,
                stop=True,
            )
            result = sb.tile([P, HALF], F32, name="result%d" % h)
            nc.scalar.copy(result[:], acc[:])
            nc.sync.dma_start(out[:, cols], result[:])
